import numpy as np, ml_dtypes
CORES = [10,34,74,98]
N = 4
BF = ml_dtypes.bfloat16
def gentries(a):
    return np.ascontiguousarray(a.reshape(8, 16, -1).transpose(0, 2, 1)).reshape(8, -1)
def gtable(e):
    e = np.asarray(e); return np.ascontiguousarray(e.reshape(8, -1, 16).transpose(0, 2, 1)).reshape(128, -1).astype(np.int32)
V, G, B, L, RO = 2048, 256, 1, 128, 3
W = V + B * G
def numbers(rng, ghost):
    s = (N, 8, V, 16)
    return np.where(rng.random(s) < ghost, rng.integers(V, W, s), rng.integers(0, V, s))
def image(t, nb):
    tw = np.concatenate([t, np.broadcast_to(np.arange(V, W), (N, 8, W - V))], axis=2)
    e = np.take_along_axis(tw, nb.reshape(N, 8, -1), 2).reshape(nb.shape)
    return np.take_along_axis(e, np.argsort(t, axis=-1)[..., None], 2)
def parts(rng, z, wild, mix):
    t = np.argsort(rng.random((N, 8, V)), axis=-1); nb = numbers(rng, 0.125)
    nz = np.where(rng.random(nb.shape) < wild, numbers(rng, 0.125), image(t, nb))
    x = np.clip(np.take_along_axis(z, t[:, :, None, :], 3) + rng.integers(-2, 3, z.shape), 0, 255)
    x = np.where(rng.random(z.shape) < 0.1, rng.integers(0, 256, z.shape), x)
    o = np.argsort(rng.random((N, 8, V)), axis=-1); m = t.copy()
    for r in range(N):
        for g in range(8):
            j = o[r, g, :int(V * mix[r, g])]; m[r, g, j] = t[r, g, np.roll(j, 1)]
    bx = np.ascontiguousarray(np.argsort(rng.random((N, 8, V)), axis=-1)[..., :G]); bz = np.take_along_axis(t, bx, 2)
    return {"x": x, "z": z, "nb": nb, "nz": nz, "m": m, "bx": bx, "bz": bz}
def pack(d):
    return {"x": np.ascontiguousarray(d["x"].reshape(N, 128, V)).astype(np.float32).astype(BF), "z": np.ascontiguousarray(d["z"].reshape(N, 128, V)).astype(np.float32).astype(BF),
            "nb": np.stack([gtable(a.reshape(8, -1)) for a in d["nb"]]), "nz": np.stack([gtable(a.reshape(8, -1)) for a in d["nz"]]),
            "m": d["m"].astype(np.int32), "im": np.argsort(d["m"], axis=-1).astype(np.int32),
            "bx": np.stack([gtable(a) for a in d["bx"]]), "bz": np.stack([gtable(a) for a in d["bz"]])}
def setup_inputs(rng):
    size = rng.permuted(np.tile(np.array([1, 1, 3, 3, 15, 63, 255, 255]), (N, 1)), axis=1)[:, :, None, None]
    z = rng.integers(0, size + 1, (N, 8, 16, V))
    wild = rng.choice(np.array([0.05, 0.2, 0.5, 1.0]), (N, 8, 1, 1)); mix = rng.choice(np.array([0.1, 0.3, 0.6, 1.0]), (N, 8))
    h = int(rng.integers(0, 8)); wild[:, h] = 0.0; mix[:, h] = 0.05
    return pack(parts(rng, z, wild, mix))
def setup_inputs_ties(rng):
    z = rng.integers(0, 2, (N, 8, 16, V)) * (rng.random((N, 8, 1, V)) < 0.5); z[:, 1, 1:] = 0
    d = parts(rng, z, rng.choice(np.array([0.2, 1.0]), (N, 8, 1, 1)), np.full((N, 8), 0.8))
    u = (np.arange(L) * (V // L))[1::2]
    for r in range(N):
        for g in (0, 2, 4, 6):
            s0 = np.flatnonzero(np.all(z[r, g] == 0, axis=0)); im = np.argsort(d["m"][r, g])
            d["nb"][r, g, u] = im[rng.choice(s0, (len(u), 16))]; d["nz"][r, g, d["m"][r, g, u]] = rng.choice(s0, (len(u), 16))
    d["nb"][:, 5] = rng.integers(0, V, (N, 1, 16))
    return pack(d)
def setup_inputs_crowd(rng):
    z = rng.integers(0, rng.choice(np.array([3, 15, 255]), (N, 8, 1, 1)) + 1, (N, 8, 16, V))
    d = parts(rng, z, np.ones((N, 8, 1, 1)), np.ones((N, 8)))
    for r in range(N):
        for g in range(8):
            n = (24, 160)[g % 2]
            s = np.concatenate([np.array([0, V - 1]), 1 + rng.permutation(V - 2)[:n - 2]]); e = np.concatenate([np.array([0, V - 1]), 1 + rng.permutation(V - 2)[:n - 2]])
            if g < 4: e = d["m"][r, g, s]
            ends = np.array([V, W - 1])
            d["nb"][r, g] = np.where(rng.random((V, 16)) < 0.05, rng.choice(ends, (V, 16)), rng.choice(s, (V, 16)))
            d["nz"][r, g] = np.where(rng.random((V, 16)) < 0.05, rng.choice(ends, (V, 16)), rng.choice(e, (V, 16)))
            d["bx"][r, g] = rng.choice(s, G); d["bz"][r, g] = rng.choice(e, G)
    return pack(d)
def setup_inputs_border(rng):
    z = rng.integers(0, rng.choice(np.array([3, 15, 255]), (N, 8, 1, 1)) + 1, (N, 8, 16, V))
    d = parts(rng, z, np.ones((N, 8, 1, 1)), np.ones((N, 8)))
    for r in range(N):
        for g in range(8):
            s = rng.permutation(V)[:160]; e = d["m"][r, g, s]
            d["nb"][r, g] = np.where(rng.random((V, 16)) < 0.3, rng.integers(V, W, (V, 16)), rng.choice(s, (V, 16)))
            d["nz"][r, g] = np.where(rng.random((V, 16)) < 0.3, rng.integers(V, W, (V, 16)), rng.choice(e, (V, 16)))
            d["bx"][r, g] = rng.choice(s, G); d["bz"][r, g] = rng.choice(e, G)
    d["bx"][:, :, 0] = 0; d["bx"][:, :, G - 1] = V - 1; d["bz"][:, :, 0] = V - 1; d["bz"][:, :, G - 1] = 0
    q = rng.permutation(8); d["nb"][:, q[0]] = rng.integers(V, W, (N, V, 16)); d["nz"][:, q[1]] = rng.integers(V, W, (N, V, 16))
    d["nb"][:, :, 0, :2] = np.array([V, W - 1])
    return pack(d)
def agree(d, r, g):
    t = np.concatenate([d["m"][r, g], np.arange(V, W)]); d["nz"][r, g, t[:V]] = t[d["nb"][r, g]]
def early(rng, d, r, g, n):
    st = np.arange(L) * (V // L); o = rng.permutation(np.setdiff1d(np.arange(V), np.concatenate([st, d["bx"][r, g]])))
    p = o[:2 * n]; a = d["nb"][r, g][st]; a[np.isin(a, p)] = o[2 * n]
    a[rng.permutation(L)[:n], rng.integers(0, 16, n)] = p[:n]; d["nb"][r, g, st] = a
    agree(d, r, g); t = d["m"][r, g].copy(); d["m"][r, g, p] = t[np.roll(p, n)]
def late(rng, d, r, g):
    st = np.arange(L) * (V // L); o = rng.permutation(np.setdiff1d(np.arange(V), np.concatenate([st, d["bx"][r, g], np.array([819, V - 1])])))
    p = o[:6].copy(); s = p[:3]; f = int(o[6]); b = o[7:7 + L].copy(); c = o[7 + L:7 + 2 * L].copy(); rest = o[7 + 2 * L:]
    j = 1 + rng.permutation(L - 1)[:3]; b[j[0]] = 819
    nb = d["nb"][r, g]; nb[np.isin(nb, p)] = f
    nb[p] = rng.choice(rest, (6, 16)); nb[s, rng.integers(0, 16, 3)] = f
    nb[st, 0] = b; nb[b, 0] = c; nb[819, 0] = rng.integers(V, W)
    nb[np.array([b[j[1]], c[j[2]], V - 1]), rng.integers(1, 16, 3)] = s
    agree(d, r, g); t = d["m"][r, g].copy(); z = d["z"][r, g]
    z[:] = rng.integers(0, 200, (16, 1)); z[:, t[s]] += rng.integers(1, 5, (16, 3)); z[int(rng.integers(0, 16)), t[f]] += rng.integers(1, 16)
    d["m"][r, g, p] = t[np.roll(p, 3)]
def setup_inputs_still(rng):
    z = rng.integers(0, 256, (N, 8, 16, V)); d = parts(rng, z, np.zeros((N, 8, 1, 1)), np.zeros((N, 8)))
    q, q2, q3 = [int(i) for i in rng.permutation(N)[:3]]; h, h2 = [int(i) for i in rng.permutation(8)[:2]]; st = np.arange(L) * (V // L)
    room = [L] + [(287 - L + i) // 5 for i in range(5)]
    for r in range(N):
        for g in range(8):
            if r == q or g == h: continue
            if r in (q2, q3):
                if g == h2: late(rng, d, r, g)
                elif r == q3: early(rng, d, r, g, room.pop())
                continue
            c = np.unique(d["nb"][r, g, st]); c = np.setdiff1d(c[c < V], np.concatenate([st, d["bx"][r, g]]))
            p = rng.permutation(c)[:2 * int(rng.integers(1, 4))]
            d["m"][r, g, p] = d["m"][r, g, p.reshape(-1, 2)[:, ::-1].reshape(-1)]
    return pack(d)
def setup_inputs_spread(rng):
    z = (np.exp2(8 * rng.random((N, 8, 1, V))) * rng.random((N, 8, 16, V)) * (rng.random((N, 8, 1, V)) > 0.0625)).astype(np.int64)
    wild = rng.choice(np.array([0.05, 0.3, 1.0]), (N, 8, 1, 1)); mix = rng.choice(np.array([0.2, 0.5, 1.0]), (N, 8))
    for h in rng.permutation(8)[:2]:
        u = rng.integers(0, 4, (N, 16, V)); z[:, h] = np.where(rng.random((N, 1, V)) < 0.5, u, 255 - u); wild[:, h] = 1.0; mix[:, h] = 1.0
    return pack(parts(rng, z, wild, mix))
def check_inputs(d):
    bad = []
    for k in ("x", "z"):
        a = np.asarray(d[k]).astype(np.float32)
        if not np.all((a >= 0) & (a <= 255) & (a == np.floor(a))): bad.append("whole numbers 0 to 255 in " + k)
    for k, hi in (("nb", W - 1), ("nz", W - 1), ("m", V - 1), ("im", V - 1), ("bx", V - 1), ("bz", V - 1)):
        if np.min(d[k]) < 0 or np.max(d[k]) > hi: bad.append("range of " + k)
    if not np.all(np.sort(d["m"], axis=-1) == np.arange(V)): bad.append("m is a bijection")
    elif not np.all(np.argsort(d["m"], axis=-1) == d["im"]): bad.append("im is the inverse of m")
    return bad
def reference(x, z, nb, nz, m, im, bx, bz):
    X = x.astype(np.float32).astype(np.int64).reshape(N, 8, 16, V); Z = z.astype(np.float32).astype(np.int64).reshape(N, 8, 16, V)
    nv = np.stack([gentries(a) for a in nb]).astype(np.int64).reshape(N, 8, V, 16); ns = np.stack([gentries(a) for a in nz]).astype(np.int64).reshape(N, 8, V, 16)
    M = m.astype(np.int64); I = im.astype(np.int64)
    b1 = np.stack([gentries(a) for a in bx]).astype(np.int64); b2 = np.stack([gentries(a) for a in bz]).astype(np.int64)
    lane = np.arange(L); v = np.tile(lane * (V // L), (N, 8, 1)); last = np.zeros(N, np.int64)
    for rnd in range(RO):
        Y = np.take_along_axis(Z, M[:, :, None, :], 3)
        ey = np.take_along_axis(Y, b1[:, :, None, :], 3); ez = np.take_along_axis(Z, b2[:, :, None, :], 3)
        YW = np.concatenate([Y] + [np.roll(ey, -d, axis=0) for d in range(1, B + 1)], axis=3)
        ZW = np.concatenate([Z] + [np.roll(ez, -d, axis=0) for d in range(1, B + 1)], axis=3)
        th = last & 31; last = np.zeros(N, np.int64)
        for r in range(N):
            for g in range(8):
                Yg, Zg, n1, n2, at = YW[r, g], ZW[r, g], nv[r, g], ns[r, g], v[r, g].copy()
                na = n1[at]; nq = n2[M[r, g, at]]
                D = np.add.reduce(np.abs(Yg[:, na] - Zg[:, nq]), axis=0); k = np.argmax(D, axis=1)
                a = na[lane, k]; q = nq[lane, k]; live = (D[lane, k] > 0) & (a < V) & (q < V)
                ac = np.minimum(a, V - 1); qc = np.minimum(q, V - 1); w = I[r, g, qc]; p = M[r, g, ac]
                Aa = Yg[:, n1[ac]]; Aw = Yg[:, n1[w]]; Ba = Zg[:, n2[p]]; Bw = Zg[:, n2[qc]]
                gain = np.add.reduce(np.abs(Aa - Ba) + np.abs(Aw - Bw) - np.abs(Aa - Bw) - np.abs(Aw - Ba), axis=(0, 2))
                prop = live & (gain > th[r])
                first = np.full(V, L); np.minimum.at(first, ac[prop], lane[prop]); np.minimum.at(first, w[prop], lane[prop])
                com = prop & (first[ac] >= lane) & (first[w] >= lane)
                last[r] += np.count_nonzero(com)
                v[r, g] = np.where(com, a, np.where(q < V, w, (5 * at + 1) & (V - 1)))
                a, w, p, q = a[com], w[com], p[com], q[com]
                M[r, g, a] = q; M[r, g, w] = p; I[r, g, q] = a; I[r, g, p] = w
                for vert, site in ((a, q), (w, p)):
                    old = Z[r, g][:, site]; Z[r, g][:, site] = old + np.clip(X[r, g][:, vert] - old, -1, 1)
    return {"mo": M.astype(np.float32), "zo": Z.reshape(N, 128, V).astype(np.float32).astype(BF)}

from concourse.mybir import AluOpType as Op, AxisListType, ActivationFunctionType as Fn

V, NB, L, RO = 2048, 256, 128, 3
WIN = NB + V + NB
CH = [(0, 32), (32, 64), (64, 96), (96, 128)]
SCH = [(64, 96), (96, 128)]
VCH = [(0, 32), (32, 64)]
DS = [(48, 64), (64, 112), (112, 128)]
DV = [(0, 32), (32, 48)]
DCH = [(0, 32), (32, 64), (64, 96), (96, 112)]
DY = (112, 128)
DP = 64
WD = 510.0
PASS = float(2 ** 40)
FAR = 1.0e6

_B, _F, _H, _I, _U = "bfloat16", "float32", "float16", "int32", "uint16"
SCRATCH = {}
for _n, _w, _t in [
    ("nbt", V, _I), ("nzt", V, _I), ("xt", V, _B),
    ("z1", WIN, _B), ("z2", WIN, _B), ("z3", WIN, _B), ("y1", WIN, _B), ("y2", WIN, _B), ("y3", WIN, _B),
    ("mt", NB + V, _F), ("it", NB + V, _F),
    ("ml32", 128, _I), ("mlh", 128, _H), ("mlt", 128, _H), ("mlist", 128, _U),
    ("m2", 128, _I), ("i2", 128, _I), ("m2h", 128, _H), ("i2h", 128, _H),
    ("bx32", 16, _I), ("bz32", 16, _I), ("bxl", 16, _U), ("bzl", 16, _U),
    ("gz", NB, _B), ("gy", NB, _B),
    ("ones", 128, _B), ("idn", 128, _B), ("idm", 128, _B), ("bo8", 8, _B), ("gp", 8, _B), ("g1", 8, _B), ("gm", 8, _B),
    ("fk", 2048, _B), ("au", 512, _B), ("auq", 256, _B), ("ej", 2048, _B),
    ("bq0", 128, _B), ("bq", 128, _B), ("lj", 16, _F), ("lk", 16, _F),
    ("tb0", 128, _B), ("tb", 128, _B), ("w1k", 1024, _B), ("dw", 1024, _B),
    ("ms0", 72, _F), ("ms1", 72, _F), ("ms", 72, _F), ("c0", 128, _F), ("c1", 128, _F),
    ("pi", 8, _I), ("pi2", 8, _I), ("pf", 8, _F), ("li", 16, _F), ("alt", 40, _F),
    ("vl", 8, _U), ("vf", 8, _F), ("mvr", 128, _H), ("mvt", 128, _H), ("mvl", 8, _U),
    ("nbv", 128, _U), ("nzv", 128, _U), ("cat", 256, _H), ("catt", 256, _H),
    ("zg", 2048, _B), ("dd", 2048, _B), ("rr", 2048, _B),
    ("db", 128, _F), ("old", 128, _H), ("s0", 256, _H), ("sc", 256, _H), ("sct", 256, _H),
    ("l4", 32, _U), ("l4f", 32, _F), ("wp", 256, _H), ("wpt", 256, _H), ("raq", 256, _F), ("nm", 256, _H),
    ("nba", 128, _U), ("nzq", 128, _U), ("nbw", 128, _U), ("nzp", 128, _U),
    ("ga", 2048, _B), ("gw", 2048, _B), ("gb", 2048, _B),
    ("m_1", 2048, _B), ("m_2", 2048, _B), ("m_3", 2048, _B), ("m_4", 2048, _B),
    ("ka", 2048, _B), ("kw", 2048, _B), ("tc", 1024, _B), ("tk", 1024, _B),
    ("xg", 256, _B), ("zd", 256, _B), ("zc", 256, _B), ("zn", 256, _B),
    ("lv0", 8, _F), ("lv1", 8, _F), ("lv2", 8, _F), ("lv", 8, _B), ("thl", 8, _F), ("thm", 8, _F), ("thn", 8, _F), ("prop", 16, _B),
    ("t6", 8, _F), ("sel", 72, _F), ("com", 40, _F), ("cm", 40, _F), ("off", 32, _U), ("n5", 40, _F), ("dl", 40, _F),
    ("sv", 8, _I), ("sv2", 8, _I), ("qo", 8, _F), ("dws", 8, _F), ("dwq", 8, _F), ("cb", 8, _B),
    ("cn", 8, _F), ("cni", 8, _I), ("cnj", 8, _I),
]:
    SCRATCH[_n] = ("sbuf", [128, _w], _t)
for _n in ["p_a", "p_b", "p_d", "p_g", "p_l", "p_q", "p_t0", "p_t1"]:
    SCRATCH[_n] = ("psum", [128, 512], "float32")

DMAS = ["d_ml", "d_z", "d_bz", "d_bx", "d_m2", "d_i2", "d_nb", "d_nz", "d_x", "d_z2", "d_y2", "d_z3", "d_y3", "d_mo", "d_zo"]
SEMAPHORES = ["V", "S", "P", "G"] + DMAS + ["%s%s%d" % (k, w, t) for k in ("arr", "snt") for w in ("z", "y") for t in (1, 2, 3)]


def rank_program(g, core, T, topo):
    rank = T.rank_of(core)
    if rank is None:
        return
    n = len(T.cores)
    dst = T.cores[(rank - 1) % n]
    rid, pid = topo.addr(dst)[:2]
    nout = len(topo.engines(core, dst))
    nin = len(topo.engines(T.cores[(rank + 1) % n], core))

    Q = {"V": g.vector, "S": g.scalar, "P": g.tensor, "G": g, "Y": g.sync}
    count = {"V": 0, "S": 0, "P": 0, "G": 0}
    known = {q: {} for q in Q}
    clock = {}
    acc = {}

    def psum(name):
        return name[:2] == "p_"

    def meet(r1, r2):
        if r1[1] >= r2[2] or r2[1] >= r1[2] or r1[3] >= r2[4] or r2[3] >= r1[4]:
            return False
        s = r1[5]
        return not (s == r2[5] and s > 1 and (r1[3] - r2[3]) % s)

    def order(q, reads, writes, me):
        need = {}
        for kind, regs in (("r", reads), ("w", writes)):
            for r in regs:
                for (e, k2, r2), idx in acc.get(r[0], {}).items():
                    same = e == q
                    if same and (q == "P" or k2 == "r"):
                        continue
                    if same or not psum(r[0]):
                        if (kind == "r" and k2 == "r") or not meet(r, r2):
                            continue
                    if need.get(e, 0) < idx:
                        need[e] = idx
        kn = known[q]
        for e in sorted(need, key=lambda e: -len(clock.get((e, need[e]), {}))):
            if kn.get(e, 0) >= need[e]:
                continue
            Q[q].wait_ge(T.sem[e], need[e])
            for e2, i2 in clock.get((e, need[e]), {}).items():
                if kn.get(e2, 0) < i2:
                    kn[e2] = i2
            kn[e] = max(kn.get(e, 0), need[e])
        e, idx = me
        clock[(e, idx)] = dict(kn)
        for kind, regs in (("r", reads), ("w", writes)):
            for r in regs:
                a = acc.setdefault(r[0], {})
                if kind == "w" and r[5] == 1 and not psum(r[0]):
                    for key in [k for k in a if k[2][1] >= r[1] and k[2][2] <= r[2] and k[2][3] >= r[3] and k[2][4] <= r[4] and k[0] != e]:
                        if kn.get(key[0], 0) >= a[key]:
                            del a[key]
                a[(e, kind, r)] = idx

    def R(name, c0=0, c1=None, step=1, p0=0, p1=128):
        return (name, p0, p1, c0, SCRATCH[name][1][1] if c1 is None else c1, step)

    def ap(r):
        if r[0] == "ind":
            return ap(r[1]).indirect(ap(r[2]))
        t = T[r[0]]
        return t[r[1]:r[2], r[3]:r[4]] if r[5] == 1 else t[r[1]:r[2], r[3]:r[4]:r[5]]

    def ind(w, o):
        return ("ind", w, o)

    def split(outs, ins):
        rd, wr = [], []
        for r in outs:
            if r[0] == "ind":
                wr.append(r[1])
                rd.append(r[2])
            else:
                wr.append(r)
        for r in ins:
            if r[0] == "ind":
                rd += [r[1], r[2]]
            else:
                rd.append(r)
        return rd, wr

    def run(q, outs, ins, call):
        rd, wr = split(outs, ins)
        count[q] += 1
        order(q, rd, wr, (q, count[q]))
        call(Q[q]).then_inc(T.sem[q], 1)

    def val(s):
        return ap(s) if isinstance(s, tuple) else s

    def tc(o, i):
        run("V", [o], [i], lambda q: q.tensor_copy(ap(o), ap(i)))

    def tt(o, a, b, op):
        run("V", [o], [a, b], lambda q: q.tensor_tensor(ap(o), ap(a), ap(b), op))

    def ts(o, i, s1, op0, s2=None, op1=None):
        ins = [i] + [s for s in (s1, s2) if isinstance(s, tuple)]
        if op1 is None:
            run("V", [o], ins, lambda q: q.tensor_scalar(ap(o), ap(i), val(s1), None, op0))
        else:
            run("V", [o], ins, lambda q: q.tensor_scalar(ap(o), ap(i), val(s1), val(s2), op0, op1))

    def scan(o, a, b, op0, op1):
        run("V", [o], [a, b], lambda q: q.tensor_tensor_scan(ap(o), ap(a), ap(b), 0.0, op0, op1))

    def tr(o, i):
        run("V", [o], [i], lambda q: q.transpose(ap(o), ap(i)))

    def ms(o, c):
        run("V", [o], [], lambda q: q.memset(ap(o), c))

    def act(o, i, scale=1.0, fn=Fn.Copy):
        run("S", [o], [i], lambda q: q.activation(ap(o), ap(i), fn, 0.0, scale))

    def mm(o, a, b, start=True, stop=True):
        run("P", [o], [a, b], lambda q: q.matmul(ap(o), ap(a), ap(b), start, stop))

    def iota(o, pat, base, cmul, flag=True):
        if flag:
            run("G", [o], [], lambda q: q.iota(ap(o), pat, base, cmul, allow_small_or_imprecise_dtypes=True))
        else:
            run("G", [o], [], lambda q: q.iota(ap(o), pat, base, cmul))

    def aff(o, i, pat, op, fill, base, cmul):
        run("G", [o], [i], lambda q: q.affine_select(ap(o), ap(i), pat, op, fill, base, cmul))

    def dma(q, sem, pairs, total=None):
        tot = 16 * (total or len(pairs))
        for o, i in pairs:
            rd, wr = split([o] if isinstance(o, tuple) else [], [i] if isinstance(i, tuple) else [])
            order(q, rd, wr, (sem, tot))
            Q[q].dma_start(val(o), val(i)).then_inc(T.sem[sem], 16)
        count[sem] = tot

    def send(w, t, src):
        win = "%s%d" % (w, t)
        snt, arr = "snt" + win, "arr" + win
        order("G", [src], [], (snt, nout))
        g.remote_dma(T[win][:, NB + V:WIN], ap(src), T.sem[arr], T.sem[snt], pid, rid, topo.mask(core, dst))
        count[snt], count[arr] = nout, nin
        acc.setdefault(win, {})[(arr, "w", R(win, NB + V, WIN))] = nin
        clock[(arr, nin)] = {}

    def own(name):
        return R(name, NB, NB + V)

    def full(name):
        return R(name, NB, WIN)

    def park(name):
        return R(name, 0, NB + V)

    pieces = [(R("ml32", 32 * c + 16 * h, 32 * c + 16 * h + 16), T.m[h::2, 512 * c:512 * c + 512]) for c in range(4) for h in range(2)]
    dma("Y", "d_ml", pieces[:4], 8)
    dma("S", "d_ml", pieces[4:], 8)
    dma("S", "d_bz", [(R("bz32"), T.bz[:, :])])
    dma("Y", "d_m2", [(R("m2"), T.m[:, :])])
    dma("S", "d_z", [(own("z1"), T.z[:, :])])
    dma("Y", "d_bx", [(R("bx32"), T.bx[:, :])])
    dma("Y", "d_nz", [(R("nzt"), T.nz[:, :])])
    dma("S", "d_nb", [(R("nbt"), T.nb[:, :])])
    dma("Y", "d_i2", [(R("i2"), T.im[:, :])])
    dma("Y", "d_x", [(R("xt"), T.x[:, :])])

    ms(R("ones"), 1.0)
    aff(R("bo8"), R("ones", 0, 8), [[-16, 8]], Op.is_ge, 0.0, 0, 1)
    aff(R("g1"), R("bo8"), [[16, 8]], Op.is_ge, 0.0, 15, -1)
    iota(R("pi"), [[0, 8]], 0, 1, False)
    iota(R("li"), [[128, 2], [16, 8]], 0, 0)
    iota(R("lj"), [[1, 16]], 0, 0)
    aff(R("bq0"), R("ones"), [[-16, 8], [0, 16]], Op.is_ge, 0.0, 0, 1)
    aff(R("bq"), R("bq0"), [[16, 8], [0, 16]], Op.is_ge, 0.0, 15, -1)
    for u in range(2):
        aff(R("auq", 128 * u, 128 * u + 128), R("ones"), [[-32, 4], [0, 2], [-1, 16]], Op.is_equal, 0.0, -16 * u, 1)
        for h in range(2):
            k = 128 * (2 * u + h)
            aff(R("au", k, k + 128), R("auq", 128 * u, 128 * u + 128), [[0, 4], [1, 2], [0, 16]], Op.is_equal, 0.0, -h, 0)
    iota(R("tb0"), [[0, 8], [-1, 16]], 15, 0)
    ms(R("fk"), 0.0)
    ts(R("pi2"), R("pi"), 15, Op.bitwise_and)
    tc(R("pf"), R("pi2"))
    ts(R("alt", 0, 16), R("li"), R("pf", 0, 1), Op.add)
    ts(R("alt", 16, 32), R("li"), R("pf", 0, 1), Op.add)
    ts(R("vf"), R("alt", 0, 8), 16.0, Op.mult)
    tc(R("vl"), R("vf"))
    ts(R("lk"), R("lj"), R("pf", 0, 1), Op.is_equal)
    ts(R("gp"), R("g1"), 2.0, Op.mult)
    ts(R("gm"), R("g1"), -2.0, Op.mult)
    for k in range(16):
        act(R("fk", 128 * k + k, 128 * k + 128, 16), R("g1"))
    for k in range(16):
        ts(R("ej", 128 * k, 128 * k + 128), R("bq"), R("lk", k, k + 1), Op.mult)
    tc(R("mlh"), R("ml32"))
    tr(R("mlt"), R("mlh"))
    tc(R("mlist"), R("mlt"))
    tc(R("bzl"), R("bz32"))
    tc(R("bxl"), R("bx32"))
    tc(R("m2h"), R("m2"))
    act(R("gz"), ind(own("z1"), R("bzl")))
    send("z", 1, R("gz"))
    tc(R("y1", NB, NB + 1024), ind(own("z1"), R("mlist", 0, 64)))
    act(R("y1", NB + 1024, NB + V), ind(own("z1"), R("mlist", 64, 128)))
    act(R("gy"), ind(own("y1"), R("bxl")))
    send("y", 1, R("gy"))
    dma("Y", "d_z2", [(own("z2"), own("z1"))])
    dma("Y", "d_y2", [(own("y2"), own("y1"))])

    ts(R("tb"), R("tb0"), 1.0 / 2048, Op.mult)
    ms(R("c0"), FAR)
    aff(R("c1"), R("c0"), [[0, 8], [1, 16]], Op.not_equal, -1.0, 0, 0)
    ms(R("w1k"), WD)
    ms(R("ms0"), PASS)
    ms(R("t6"), FAR)
    aff(R("idn"), R("ones"), [[-1, 128]], Op.is_equal, 0.0, 0, 1)
    aff(R("ms1"), R("ms0"), [[0, 8], [-16, 9]], Op.is_ge, 1.0, 16, 1)
    aff(R("ms"), R("ms1"), [[0, 8], [16, 9]], Op.is_ge, 0.0, -1, -1)
    aff(R("dw"), R("w1k"), [[-16, 8], [0, 8], [-1, 16]], Op.is_equal, 0.0, 0, 1)

    def spread(half, tab):
        for jb in range(4):
            b = ("p_a", "p_b")[jb % 2]
            for j in range(4):
                J = 4 * jb + j
                mm(R(b, 128 * j, 128 * j + 128), R("ej", 128 * J, 128 * J + 128), R(half))
            act(R(tab, NB + 512 * jb, NB + 512 * jb + 512), R(b))

    spread("m2h", "mt")

    def lists(base, nx, src, at):
        for u in range(2):
            for h in range(2):
                k = 128 * (2 * u + h)
                mm(R("p_l", base + u, base + 8 * nx, 2), R("au", k, k + 128), R(src, 16 * h + at, 128 * nx, 32), h == 0, h == 1)

    def cols(ln):
        return 16 * ln[0], 16 * ln[1]

    for t in range(1, RO + 1):
        Y, Z = "y%d" % t, "z%d" % t
        Yn, Zn = ("y%d" % (t + 1), "z%d" % (t + 1)) if t < RO else (Y, Z)
        tc(R("mvr"), ind(own("mt"), R("vl")))
        tr(R("mvt"), R("mvr"))
        lists(0, 1, "mvt", 0)
        if t > 1:
            tc(R("nbv"), ind(R("nbt"), R("vl")))
        tc(R("mvl"), R("p_l", 0, 8))
        tc(R("nzv"), ind(R("nzt"), R("mvl")))
        if t == 1:
            ms(R("prop"), 0.0)
            ts(R("idm"), R("idn"), -1.0, Op.mult)
            tc(R("i2h"), R("i2"))
            tc(R("nbv"), ind(R("nbt"), R("vl")))
        ts(R("cat", 0, 128), R("nbv"), 2048.0, Op.min)
        ts(R("cat", 128, 256), R("nzv"), 2048.0, Op.min)
        tr(R("catt"), R("cat"))
        for ln in DS:
            act(R("zg", *cols(ln)), ind(full(Z), R("nzv", *ln)))
        for ln in DV:
            tc(R("zg", *cols(ln)), ind(full(Z), R("nzv", *ln)))
        act(R("dd", *cols(DY)), ind(full(Y), R("nbv", *DY)))
        yz = R("p_a", 0, 16 * (DY[1] - DY[0]))
        mm(yz, R("idn"), R("dd", *cols(DY)), True, False)
        mm(yz, R("idm"), R("zg", *cols(DY)), False, True)

        def sums(e):
            o = R("p_d", DP * e, DP * e + DP)
            mm(o, R("tb"), R("ones", 0, DP), True, False)
            for k in range(16):
                mm(o, R("fk", 128 * k, 128 * k + 128), R("rr", 16 * DP * e + k, 16 * DP * (e + 1), 16), False, k == 15)

        for x, ln in enumerate(DCH):
            tt(R("dd", *cols(ln)), ind(full(Y), R("nbv", *ln)), R("zg", *cols(ln)), Op.subtract)
            act(R("rr", *cols(ln)), R("dd", *cols(ln)), 1.0, Fn.Abs)
            if x == 0:
                act(R("rr", *cols(DY)), yz, 1.0, Fn.Abs)
            if ln[1] == DP:
                sums(0)
        sums(1)
        if t > 1:
            tc(ind(park("it"), R("off", 0, 8)), R("raq", 0, 128))
            tc(ind(park("it"), R("off", 8, 16)), R("wp", 0, 128))
            tc(R("cb"), R("com", 0, 8))
            mm(R("p_l", 80, 88), R("ones"), R("cb"))
            run("V", [R("cn", 0, 1)], [R("p_l", 80, 88)],
                lambda q: q.tensor_reduce(ap(R("cn", 0, 1)), ap(R("p_l", 80, 88)), AxisListType.X, Op.add))
            tc(R("cni", 0, 1), R("cn", 0, 1))
            ts(R("cnj", 0, 1), R("cni", 0, 1), 31, Op.bitwise_and)
            ts(R("t6", 0, 1), R("cnj", 0, 1), FAR, Op.add)
        else:
            spread("i2h", "it")
            ms(R("ka"), 0.0)
            ms(R("kw"), 0.0)
        tr(R("db"), R("p_d", 0, 128))
        scan(R("p_q", 0, 128), R("c1"), R("db"), Op.min, Op.max)
        tt(R("p_q", 128, 256), R("p_q", 0, 128), R("db"), Op.is_equal)
        tt(R("old"), R("p_q", 0, 128), R("db"), Op.is_gt)
        tt(R("s0", 0, 128), R("p_q", 128, 256), R("catt", 0, 128), Op.mult)
        tt(R("s0", 128, 256), R("p_q", 128, 256), R("catt", 128, 256), Op.mult)
        scan(R("sc", 0, 128), R("old"), R("s0", 0, 128), Op.mult, Op.add)
        scan(R("sc", 128, 256), R("old"), R("s0", 128, 256), Op.mult, Op.add)
        lists(16, 2, "sc", 15)
        ts(R("l4", 0, 8), R("p_l", 16, 24), 2047.0, Op.min)
        ts(R("l4", 16, 24), R("p_l", 24, 32), 2047.0, Op.min)
        tc(R("nba"), ind(R("nbt"), R("l4", 0, 8)))
        tc(R("wp", 0, 128), ind(own("it"), R("l4", 16, 24)))
        tc(R("wp", 128, 256), ind(own("mt"), R("l4", 0, 8)))
        tr(R("wpt"), R("wp"))
        lists(32, 2, "wpt", 0)
        tc(R("nzq"), ind(R("nzt"), R("l4", 16, 24)))
        tr(R("sct"), R("sc"))
        mm(R("p_d", 128, 384), R("ej", 128 * 15, 2048), R("sct"))
        tc(R("l4", 8, 16), R("p_l", 32, 40))
        tc(R("l4", 24, 32), R("p_l", 40, 48))
        tc(R("nbw"), ind(R("nbt"), R("l4", 8, 16)))
        tc(R("nzp"), ind(R("nzt"), R("l4", 24, 32)))

        def fetch(o, win, lst, ln):
            act(R(o, *cols(ln)), ind(full(win), R(lst, *ln)))

        def fused(mx, src, ln):
            tt(R(mx, *cols(ln)), ind(full(Z), R("nzq", *ln)), R(src, *cols(ln)), Op.max)

        def gain(terms, o):
            for x, (mx, wgt) in enumerate(terms):
                for k in range(16):
                    mm(o, R(mx, k, 2048, 16), R(wgt), x == 0 and k == 0, x == len(terms) - 1 and k == 15)

        for ln in CH[:2]:
            fetch("ga", Y, "nba", ln)
        act(R("raq"), R("p_d", 128, 384))
        for ln in CH[2:]:
            fetch("ga", Y, "nba", ln)
        for ln in CH:
            fused("m_1", "ga", ln)
        gain([("m_1", "gm")], R("p_g", 0, 8))
        fetch("gw", Y, "nbw", CH[0])
        act(R("xg"), ind(R("xt"), R("l4", 0, 16)))
        for ln in CH[1:]:
            fetch("gw", Y, "nbw", ln)
        ts(R("l4f", 0, 8), R("p_l", 16, 24), 2047.0, Op.min)
        ts(R("l4f", 16, 24), R("p_l", 24, 32), 2047.0, Op.min)
        ts(R("qo"), R("p_l", 24, 32), 2048.0, Op.is_lt)
        tc(R("l4f", 8, 16), R("p_l", 32, 40))
        tc(R("l4f", 24, 32), R("p_l", 40, 48))
        tc(R("nm", 0, 256, 2), R("raq", 0, 128))
        tc(R("nm", 1, 256, 2), R("wp", 0, 128))
        for c in range(8):
            wd = 32 * (c + 1)
            for kk, s in (("ka", c), ("kw", 8 + c)):
                ts(R(kk, 256 * c, 256 * c + wd), R("nm", 0, wd), R("l4f", s, s + 1), Op.is_equal)
            o = R("p_t%d" % (c // 4), 128 * (c % 4), 128 * (c % 4) + 128)
            mm(o, R("idn"), R("dw", 128 * c, 128 * c + 128), True, False)
            for x, (kk, y) in enumerate((("ka", 0), ("ka", 1), ("kw", 0), ("kw", 1))):
                mm(o, R(kk, 256 * c + y, 256 * c + 256, 2), R("idn"), False, x == 3)
        tt(R("lv0"), R("sc", 15, 128, 16), R("sc", 128 + 15, 256, 16), Op.max)
        ts(R("lv1"), R("lv0"), 2048.0, Op.is_lt)
        ts(R("lv2"), R("p_q", 15, 128, 16), 1.0, Op.is_ge)
        tt(R("lv"), R("lv1"), R("lv2"), Op.mult)
        for e in range(4):
            for b in range(4):
                mm(R("p_l", 64 + 2 * b, 66 + 2 * b, 1, 32 * e, 32 * e + 32), R("idn", 32 * b, 32 * b + 32), R("lv", 2 * e, 2 * e + 2))
        for ln in CH[2:]:
            fetch("gb", Z, "nzp", ln)
        for x in range(2):
            act(R("tc", 512 * x, 512 * x + 512), R("p_t%d" % x))
        aff(R("tk"), R("tc"), [[16, 8], [0, 8], [1, 16]], Op.is_ge, 0.0, 0, -1)
        for ln in CH[:2]:
            fetch("gb", Z, "nzp", ln)
        fused("m_2", "gw", CH[0])
        if t < RO:
            ts(R("sv"), R("vf"), 5.0, Op.mult, 1.0, Op.add)
            ts(R("sv2"), R("sv"), 2047, Op.bitwise_and)
            tt(R("dws"), R("l4f", 8, 16), R("sv2"), Op.subtract)
            tt(R("dwq"), R("dws"), R("qo"), Op.mult)
            tt(R("alt", 32, 40), R("dwq"), R("sv2"), Op.add)
            tc(R("n5", 32, 40), R("l4f", 0, 8))
        ts(R("n5", 0, 16), R("l4f", 16, 32), float(NB), Op.add)
        ts(R("n5", 16, 32), R("l4f", 0, 16), float(NB), Op.add)
        wide = 40 if t < RO else 32
        tt(R("dl", 0, wide), R("n5", 0, wide), R("alt", 0, wide), Op.subtract)
        ts(R("thl"), R("p_l", 64, 72), -FAR, Op.mult, R("t6", 0, 1), Op.add)
        qp = R("l4", 16, 32)
        tt(R("zd"), ind(own(Z), qp), R("xg"), Op.subtract)
        for ln in CH[1:]:
            fused("m_2", "gw", ln)
        ts(R("zc"), R("zd"), -1.0, Op.max, 1.0, Op.min)
        tt(R("zn"), ind(own(Z), qp), R("zc"), Op.subtract)
        sb = ["p_t0", "p_t1", "p_b"]
        uses = [0]

        def on_s(ln):
            for mx, src in (("m_3", "ga"), ("m_4", "gw")):
                b = R(sb[uses[0] % 3], 0, 16 * (ln[1] - ln[0]))
                uses[0] += 1
                mm(b, R("idn"), R(src, *cols(ln)), True, False)
                mm(b, R("idm"), R("gb", *cols(ln)), False, True)
                act(R(mx, *cols(ln)), b, 1.0, Fn.Relu)

        def on_v(ln, b):
            b = R(b, 0, 16 * (ln[1] - ln[0]))
            mm(b, R("idn"), R("gb", *cols(ln)))
            tt(R("m_3", *cols(ln)), b, R("ga", *cols(ln)), Op.max)
            tt(R("m_4", *cols(ln)), b, R("gw", *cols(ln)), Op.max)

        on_s(SCH[0])
        on_v(VCH[0], "p_a")
        on_s(SCH[1])
        on_v(VCH[1], "p_q")
        gain([("m_2", "gp")], R("p_g", 8, 16))
        tt(R("thm"), R("thl"), R("p_g", 0, 8), Op.subtract)
        tt(R("thn"), R("thm"), R("p_g", 8, 16), Op.subtract)
        gain([("m_3", "gp"), ("m_4", "gm")], R("p_d", 400, 408))
        tt(R("prop", 1, 9), R("p_d", 400, 408), R("thn"), Op.is_gt)
        for c in range(8):
            mm(R("p_d", 9 * c, 9 * c + 9), R("tk", 128 * c, 128 * c + 128), R("prop", 0, 9))
        scan(R("sel"), R("p_d", 0, 72), R("ms"), Op.max, Op.mult)
        for x in range(wide // 8):
            ts(R("com", 8 * x, 8 * x + 8), R("sel", 8, 72, 9), (WD + 2) * PASS, Op.is_equal)
        tt(R("cm", 0, wide), R("com", 0, wide), R("dl", 0, wide), Op.mult)
        tt(R("off"), R("cm", 0, 32), R("alt", 0, 32), Op.add)
        tc(ind(park(Zn), R("off", 0, 16)), R("zn"))
        if t < RO:
            act(R("gz"), ind(own(Zn), R("bzl")))
            send("z", t + 1, R("gz"))
            tc(ind(park(Yn), R("off", 16, 32)), R("zn"))
            act(R("gy"), ind(own(Yn), R("bxl")))
            send("y", t + 1, R("gy"))
            tt(R("vl"), R("cm", 32, 40), R("alt", 32, 40), Op.add)
            tt(R("vf"), R("cm", 32, 40), R("alt", 32, 40), Op.add)
        else:
            dma("Y", "d_zo", [(T.zo[:, :], own(Zn))])
        tc(ind(park("mt"), R("off", 16, 24)), R("raq", 128, 256))
        tc(ind(park("mt"), R("off", 24, 32)), R("wp", 128, 256))
        if t == 1:
            dma("Y", "d_z3", [(own("z3"), own("z2"))])
            dma("Y", "d_y3", [(own("y3"), own("y2"))])
    order("Y", [own("mt")], [], ("d_mo", 16))
    g.sync.dma_start(T.mo[:, :], T.mt[0:128:16, NB:NB + V]).then_inc(T.sem["d_mo"], 16)
    count["d_mo"] = 16

    for e in sorted(count):
        if known["G"].get(e, 0) < count[e]:
            g.wait_ge(T.sem[e], count[e])
